import numpy as np
import ml_dtypes


def mxq(x, axis, fmt="e4m3"):
    dtype, down = {"e4m3": (ml_dtypes.float8_e4m3fn, 7), "e5m2": (ml_dtypes.float8_e5m2, 14)}[fmt]
    v = np.moveaxis(np.asarray(x, np.float32).astype(ml_dtypes.bfloat16).astype(np.float64), axis, -1)
    blocks = v.reshape(v.shape[:-1] + (-1, 32))
    amax = np.abs(blocks).max(-1, keepdims=True)
    byte = np.maximum(np.where(amax > 0, np.frexp(amax)[1] - 1 + 127, 0) - down, 1)
    scale = np.exp2(byte - 127.0)
    codes = (blocks / scale).astype(np.float32).astype(dtype).astype(np.float64)
    return np.moveaxis((codes * scale).reshape(v.shape), -1, axis)


WIDE = False


def mx_kscale(k):
    if not WIDE:
        return np.ones(k)
    levels = np.array([30, -30])
    if k % 512:
        return np.exp2(np.random.permutation(np.resize(levels, k // 32))).repeat(32)
    a = np.empty((k // 512, 16))
    for p in range(k // 512):
        a[p, :8] = np.random.permutation(np.resize(levels, 8))
        for g in range(8):
            far = levels[np.abs(levels - a[p, g]) >= 10]
            a[p, g + 8] = far[np.random.randint(len(far))]
    return np.exp2(a.ravel()).repeat(32)


def f64(x):
    return np.asarray(x).astype(np.float64)


def striped(idx):
    return np.tile(np.asarray(idx).reshape(-1, 16).T, (8, 1)).astype(np.uint16)


def unstriped(offs):
    return offs[:16].T.reshape(-1).astype(np.int64)


E2M1 = np.array([0.0, 0.5, 1.0, 1.5, 2.0, 3.0, 4.0, 6.0, -0.0, -0.5, -1.0, -1.5, -2.0, -3.0, -4.0, -6.0])


def pack_weight(w, fmt):
    k, n = w.shape
    w = f64(np.asarray(w, np.float32).astype(ml_dtypes.bfloat16)).reshape(k // 32, 32, n)
    amax = np.abs(w).max(1)
    if fmt == "e4m3":
        byte = np.frexp(amax)[1] - 1 + 127 - 7
    else:
        mant, ex = np.frexp(amax / 6.0)
        byte = np.where(mant > 0.5, ex, ex - 1) + 127
    byte = np.clip(np.where(amax > 0, byte, 1), 1, 254)
    scaled = (w * np.exp2(127.0 - byte)[:, None, :]).reshape(k, n).astype(np.float32)
    by_word = np.ascontiguousarray(scaled.reshape(k // 512, 128, 4, n).transpose(0, 1, 3, 2))
    if fmt == "e4m3":
        words = by_word.astype(ml_dtypes.float8_e4m3fn).view(np.uint8)
    else:
        c = by_word.astype(ml_dtypes.float4_e2m1fn).view(np.uint8) & 0xF
        words = (c[..., 0::2] | (c[..., 1::2] << 4)).reshape(k // 512, 128, 2 * n)
    return np.ascontiguousarray(words), np.ascontiguousarray(byte.astype(np.uint8).reshape(k // 512, 16, n))


def unpack_weight(words, scales, fmt):
    g, _, n = scales.shape
    words = np.ascontiguousarray(words).reshape(g, 128, n, -1)
    if fmt == "e4m3":
        vals = words.view(ml_dtypes.float8_e4m3fn).astype(np.float64)
    else:
        nib = np.empty((g, 128, n, 4), np.uint8)
        nib[..., 0::2] = words & 0xF
        nib[..., 1::2] = words >> 4
        vals = E2M1[nib]
    vals = vals * np.repeat(np.exp2(scales.astype(np.float64) - 127.0), 8, axis=1)[..., None]
    return vals.transpose(0, 1, 3, 2).reshape(g * 512, n)


K, F, T, Z, J, R, O, N, E = 512, 512, 1024, 1024, 256, 512, 128, 256, 1024


def setup_inputs():
    n = np.random.standard_normal
    idx = np.random.permutation(T)[:J]
    idx2 = np.random.permutation(Z)[:J]
    idx3 = np.random.permutation(J)[:O]
    idx4 = np.random.permutation(T)[:O]
    idx5 = np.random.permutation(E)[:O]
    fk = mx_kscale(K)
    fr = mx_kscale(R)
    ff = mx_kscale(F)
    xtp = pack_weight(n((K, T)) / fk[:, None], "e2m1")
    wp = pack_weight(n((K, R)) * 1 / np.sqrt(K) * fk[:, None] * fr, "e4m3")
    xop = pack_weight(n((F, Z)) / ff[:, None], "e4m3")
    w2p = pack_weight(n((F, R)) * 1 / np.sqrt(F) * ff[:, None] * fr, "e2m1")
    wbp = pack_weight(n((R, N)) * 1 / np.sqrt(R) / fr[:, None], "e2m1")
    wsp = pack_weight(n((K, N)) * 1 / np.sqrt(K) * fk[:, None], "e4m3")
    return {
        "xt_words": xtp[0],
        "xt_scales": xtp[1],
        "w_words": wp[0],
        "w_scales": wp[1],
        "xo_words": xop[0],
        "xo_scales": xop[1],
        "w2_words": w2p[0],
        "w2_scales": w2p[1],
        "sa": (np.random.uniform(0.5, 1.6, (R, 1))).astype(np.float32),
        "wb_words": wbp[0],
        "wb_scales": wbp[1],
        "ws_words": wsp[0],
        "ws_scales": wsp[1],
        "tz": (np.random.randint(-9, 10, (N, E)).astype(np.float64)).astype(np.float32),
        "so": (np.random.uniform(0.1, 0.3, (N, 1))).astype(np.float32),
        "offs": striped(idx),
        "offs2": striped(idx2),
        "offs3": striped(idx3),
        "offs4": striped(idx4),
        "offs5": striped(idx5),
    }


def reference(xt_words, xt_scales, w_words, w_scales, xo_words, xo_scales, w2_words, w2_scales, sa, wb_words, wb_scales, ws_words, ws_scales, tz, so, offs, offs2, offs3, offs4, offs5):
    idx = unstriped(offs)
    idx2 = unstriped(offs2)
    idx3 = unstriped(offs3)
    idx4 = unstriped(offs4)
    idx5 = unstriped(offs5)
    xtu = unpack_weight(xt_words, xt_scales, "e2m1")
    wu = unpack_weight(w_words, w_scales, "e4m3")
    xou = unpack_weight(xo_words, xo_scales, "e4m3")
    w2u = unpack_weight(w2_words, w2_scales, "e2m1")
    wbu = unpack_weight(wb_words, wb_scales, "e2m1")
    wsu = unpack_weight(ws_words, ws_scales, "e4m3")
    xtidxg = xtu[:, idx]
    a = wu.T @ xtidxg
    xoidx2g = xou[:, idx2]
    b = w2u.T @ xoidx2g
    g1 = np.maximum(a, b)
    hid = g1[:, idx3] * f64(sa)
    hidq = mxq(hid, 0, "e5m2")
    xtidx4g = xtu[:, idx4]
    p = wbu.T @ hidq + wsu.T @ xtidx4g
    y = np.maximum(p, f64(tz)[:, idx5] * f64(so))
    return y

@@ -1,0 +1,159 @@
+from contextlib import ExitStack
+
+import concourse.mybir as mybir
+
+F32 = mybir.dt.float32
+BF16 = mybir.dt.bfloat16
+I32 = mybir.dt.int32
+U32 = mybir.dt.uint32
+U16 = mybir.dt.uint16
+U8 = mybir.dt.uint8
+E4M3X4 = mybir.dt.float8_e4m3fn_x4
+E5M2X4 = mybir.dt.float8_e5m2_x4
+E2M1X4 = mybir.dt.float4_e2m1fn_x4
+COPY = mybir.ActivationFunctionType.Copy
+MAX = mybir.AluOpType.max
+
+P = 128
+K, T, Z, J, R, O, N, E = 512, 1024, 1024, 256, 512, 128, 256, 1024
+FLOPS = 2 * K * R * J * 2 + 2 * R * N * O + 2 * K * N * O
+
+
+def load_plane(queue, plane, scales):
+    for q in range(4):
+        queue.dma_start(out=plane[32 * q : 32 * q + 4, :].bitcast(I32), in_=scales[0, 4 * q : 4 * q + 4, :].bitcast(I32))
+
+
+def words32(words):
+    return words[0].rearrange("p n t -> p (n t)").bitcast(I32)
+
+
+def deal(copy, dealt, natural, run):
+    copy(out=dealt[:].rearrange("p t (b i) -> p b t i", i=run), in_=natural[:].rearrange("p (b i t) -> p b t i", i=run, t=4))
+
+
+def tile_list_largestpicked_twotab_further_stepfloor_kernel(
+    tc, xt_words, xt_scales, w_words, w_scales, xo_words, xo_scales, w2_words, w2_scales, sa,
+    wb_words, wb_scales, ws_words, ws_scales, tz, so, offs, offs2, offs3, offs4, offs5, out,
+):
+    nc = tc.nc
+    with ExitStack() as ctx:
+        sb = ctx.enter_context(tc.tile_pool(name="sb", bufs=1))
+        ps = ctx.enter_context(tc.psum_pool(name="ps", bufs=1))
+
+        l1 = sb.tile([P, J // 16], U16, name="l1")
+        l2 = sb.tile([P, J // 16], U16, name="l2")
+        l3 = sb.tile([P, O // 16], U16, name="l3")
+        l4 = sb.tile([P, O // 16], U16, name="l4")
+        l5 = sb.tile([P, O // 16], U16, name="l5")
+        xtw = sb.tile([P, T], U16, name="xtw", align_bytes=64)
+        xts = sb.tile([P, T], U8, name="xts", align_bytes=64)
+        xow = sb.tile([P, Z], U32, name="xow", align_bytes=64)
+        xos = sb.tile([P, Z], U8, name="xos", align_bytes=64)
+        ww = sb.tile([P, R], U32, name="ww", align_bytes=64)
+        wsc = sb.tile([P, R], U8, name="wsc", align_bytes=64)
+        w2w = sb.tile([P, R], U16, name="w2w", align_bytes=64)
+        w2sc = sb.tile([P, R], U8, name="w2sc", align_bytes=64)
+        wbw = sb.tile([P, N], U16, name="wbw", align_bytes=64)
+        wbsc = sb.tile([P, N], U8, name="wbsc", align_bytes=64)
+        wsw = sb.tile([P, N], U32, name="wsw", align_bytes=64)
+        wssc = sb.tile([P, N], U8, name="wssc", align_bytes=64)
+        sa_t = sb.tile([P, 4], F32, name="sa_t")
+        so_t = sb.tile([P, 2, 1], F32, name="so_t")
+        tz_t = [sb.tile([P, E], F32, name="tz%d" % h) for h in range(2)]
+
+        for plane in (xts, wsc, xos, w2sc):
+            nc.vector.memset(plane[:].bitcast(I32), 0)
+        for plane in (wssc, wbsc):
+            nc.gpsimd.memset(plane[:].bitcast(I32), 0)
+
+        nc.sync.dma_start(l1[:], offs)
+        nc.sync.dma_start(out=xtw[:].bitcast(I32), in_=xt_words[0].bitcast(I32))
+        load_plane(nc.scalar, xts, xt_scales)
+        nc.sync.dma_start(out=ww[:].bitcast(I32), in_=words32(w_words))
+        nc.sync.dma_start(out=xow[:].bitcast(I32), in_=words32(xo_words))
+        load_plane(nc.scalar, wsc, w_scales)
+        nc.sync.dma_start(l2[:], offs2)
+        load_plane(nc.sync, xos, xo_scales)
+        nc.sync.dma_start(out=w2w[:].bitcast(I32), in_=w2_words[0].bitcast(I32))
+        load_plane(nc.sync, w2sc, w2_scales)
+        nc.sync.dma_start(l3[:], offs3)
+        nc.sync.dma_start(l4[:], offs4)
+        for h in range(2):
+            nc.sync.dma_start(out=tz_t[h][:], in_=tz[P * h : P * (h + 1), :])
+        nc.sync.dma_start(out=wsw[:].bitcast(I32), in_=words32(ws_words))
+        nc.sync.dma_start(out=wbw[:].bitcast(I32), in_=wb_words[0].bitcast(I32))
+        nc.sync.dma_start(l5[:], offs5)
+        with nc.allow_non_contiguous_dma(reason="one value a partition and half"):
+            nc.sync.dma_start(out=so_t[:], in_=so.rearrange("(h p) o -> p h o", h=2))
+        load_plane(nc.sync, wbsc, wb_scales)
+        nc.gpsimd.dma_start(out=sa_t[:], in_=sa.rearrange("(p t) o -> p (t o)", t=4))
+        load_plane(nc.gpsimd, wssc, ws_scales)
+
+        xtw_g = sb.tile([P, J], U16, name="xtw_g", align_bytes=64)
+        xts_g = sb.tile([P, J], U8, name="xts_g", align_bytes=64)
+        xow_g = sb.tile([P, J], U32, name="xow_g", align_bytes=64)
+        xos_g = sb.tile([P, J], U8, name="xos_g", align_bytes=64)
+        xtw_g4 = sb.tile([P, O], U16, name="xtw_g4", align_bytes=64)
+        xts_g4 = sb.tile([P, O], U8, name="xts_g4", align_bytes=64)
+        ww_d = sb.tile([P, 4, P], U32, name="ww_d", align_bytes=64)
+        wsc_d = sb.tile([P, 4, P], U8, name="wsc_d", align_bytes=64)
+        w2w_d = sb.tile([P, 4, P], U16, name="w2w_d", align_bytes=64)
+        w2sc_d = sb.tile([P, 4, P], U8, name="w2sc_d", align_bytes=64)
+
+        nc.vector.tensor_copy(xtw_g[:], xtw[:].indirect(l1[:]))
+        nc.vector.tensor_copy(xts_g[:], xts[:].indirect(l1[:]))
+        deal(nc.scalar.copy, ww_d, ww, 4)
+        deal(nc.vector.tensor_copy, wsc_d, wsc, 16)
+        a_ps = [ps.tile([P, 2, J], F32, name="a_ps%d" % u) for u in range(2)]
+        a_sb = [sb.tile([P, 2, J], F32, name="a_sb%d" % u) for u in range(2)]
+        for t in range(4):
+            nc.tensor.matmul_mx(
+                out=a_ps[t // 2][:, t % 2, :], lhsT=ww_d[:, t, :].bitcast(E4M3X4), lhsT_scale=wsc_d[:, t, :],
+                rhs=xtw_g[:].bitcast(E2M1X4), rhs_scale=xts_g[:], start=True, stop=True)
+        deal(nc.scalar.copy, w2w_d, w2w, 8)
+        for u in range(2):
+            nc.scalar.copy(out=a_sb[u][:], in_=a_ps[u][:])
+
+        nc.vector.tensor_copy(xow_g[:], xow[:].indirect(l2[:]))
+        nc.vector.tensor_copy(xos_g[:], xos[:].indirect(l2[:]))
+        deal(nc.vector.tensor_copy, w2sc_d, w2sc, 16)
+        b_ps = [ps.tile([P, J], F32, name="b_ps%d" % t) for t in range(4)]
+        g1 = [sb.tile([P, J], F32, name="g1_%d" % t) for t in range(4)]
+        hid = sb.tile([P, 4, O], BF16, name="hid", align_bytes=64)
+        for t in range(4):
+            nc.tensor.matmul_mx(
+                out=b_ps[t][:], lhsT=w2w_d[:, t, :].bitcast(E2M1X4), lhsT_scale=w2sc_d[:, t, :],
+                rhs=xow_g[:].bitcast(E4M3X4), rhs_scale=xos_g[:], start=True, stop=True)
+        for t in range(4):
+            nc.vector.tensor_tensor(g1[t][:], b_ps[t][:], a_sb[t // 2][:, t % 2, :], MAX)
+            nc.scalar.activation(out=hid[:, t, :], in_=g1[t][:].indirect(l3[:]), func=COPY, scale=sa_t[:, t : t + 1])
+
+        nc.vector.tensor_copy(xtw_g4[:], xtw[:].indirect(l4[:]))
+        nc.vector.tensor_copy(xts_g4[:], xts[:].indirect(l4[:]))
+        p_ps = [ps.tile([P, O], F32, name="p_ps%d" % h) for h in range(2)]
+        for h in range(2):
+            cols = slice(P * h, P * (h + 1))
+            nc.tensor.matmul_mx(
+                out=p_ps[h][:], lhsT=wsw[:, cols].bitcast(E4M3X4), lhsT_scale=wssc[:, cols],
+                rhs=xtw_g4[:].bitcast(E2M1X4), rhs_scale=xts_g4[:], start=True, stop=False)
+
+        woven = sb.tile([P, O, 4], BF16, name="woven", align_bytes=64)
+        nc.vector.tensor_copy(
+            out=woven[:].rearrange("p (c i) t -> p c t i", i=4), in_=hid[:].rearrange("p t (c i) -> p c t i", i=4))
+        hq = sb.tile([P, O], U32, name="hq", align_bytes=64)
+        hs = sb.tile([P, O], U8, name="hs", align_bytes=64)
+        nc.vector.quantize_mx(out=hq[:].bitcast(E5M2X4), scales=hs[:], in_=woven[:].rearrange("p o t -> p (o t)"))
+
+        floor_t = [sb.tile([P, O], F32, name="floor%d" % h) for h in range(2)]
+        res = [sb.tile([P, O], F32, name="res%d" % h) for h in range(2)]
+        for h in range(2):
+            nc.scalar.activation(out=floor_t[h][:], in_=tz_t[h][:].indirect(l5[:]), func=COPY, scale=so_t[:, h, :])
+        for h in range(2):
+            cols = slice(P * h, P * (h + 1))
+            nc.tensor.matmul_mx(
+                out=p_ps[h][:], lhsT=wbw[:, cols].bitcast(E2M1X4), lhsT_scale=wbsc[:, cols],
+                rhs=hq[:].bitcast(E5M2X4), rhs_scale=hs[:], start=False, stop=True)
+        for h, queue in enumerate((nc.sync, nc.scalar)):
+            nc.vector.tensor_tensor(res[h][:], p_ps[h][:], floor_t[h][:], MAX)
+            queue.dma_start(out=out[P * h : P * (h + 1), :], in_=res[h][:])

@@ -24,12 +24,26 @@ def load_plane(queue, plane, scales):
         queue.dma_start(out=plane[32 * q : 32 * q + 4, :].bitcast(I32), in_=scales[0, 4 * q : 4 * q + 4, :].bitcast(I32))
 
 
+def load_half(queue, pair, cols, scales, q):
+    by_quadrant = scales[0].rearrange("(b q r) c -> q r b c", b=2, q=2)
+    queue.dma_start(out=pair[32 * q : 32 * q + 4, :, cols].bitcast(I32), in_=by_quadrant[q].bitcast(I32))
+
+
+def load_halves(queues, pair, cols, scales):
+    for q, queue in enumerate(queues):
+        load_half(queue, pair, cols, scales, q)
+
+
+def lift(nc, pair):
+    nc.vector.tensor_copy(out=pair[64:128, 0, :].bitcast(I32), in_=pair[0:64, 1, :].bitcast(I32))
+
+
 def words32(words):
     return words[0].rearrange("p n t -> p (n t)").bitcast(I32)
 
 
 def deal(copy, dealt, natural, run):
-    copy(out=dealt[:].rearrange("p t (b i) -> p b t i", i=run), in_=natural[:].rearrange("p (b i t) -> p b t i", i=run, t=4))
+    copy(out=dealt[:].rearrange("p t (b i) -> p b t i", i=run), in_=natural.rearrange("p (b i t) -> p b t i", i=run, t=4))
 
 
 def tile_list_largestpicked_twotab_further_stepfloor_kernel(
@@ -48,47 +62,48 @@ def tile_list_largestpicked_twotab_further_stepfloor_kernel(
         l5 = sb.tile([P, O // 16], U16, name="l5")
         xtw = sb.tile([P, T], U16, name="xtw", align_bytes=64)
         xts = sb.tile([P, T], U8, name="xts", align_bytes=64)
+        xts_pair = sb.tile([64, 2, T // 4], I32, name="xts_pair")
         xow = sb.tile([P, Z], U32, name="xow", align_bytes=64)
         xos = sb.tile([P, Z], U8, name="xos", align_bytes=64)
         ww = sb.tile([P, R], U32, name="ww", align_bytes=64)
-        wsc = sb.tile([P, R], U8, name="wsc", align_bytes=64)
-        w2w = sb.tile([P, R], U16, name="w2w", align_bytes=64)
-        w2sc = sb.tile([P, R], U8, name="w2sc", align_bytes=64)
+        wsc = sb.tile([P, 2, R], U8, name="wsc", align_bytes=64)
+        w2w = sb.tile([P, R], U16, name="w2w", tag="w2w_then_a", align_bytes=64)
+        w2sc = sb.tile([P, 2, R], U8, name="w2sc", align_bytes=64)
         wbw = sb.tile([P, N], U16, name="wbw", align_bytes=64)
-        wbsc = sb.tile([P, N], U8, name="wbsc", align_bytes=64)
         wsw = sb.tile([P, N], U32, name="wsw", align_bytes=64)
-        wssc = sb.tile([P, N], U8, name="wssc", align_bytes=64)
+        osc = sb.tile([P, 2, 2 * N], U8, name="osc", align_bytes=64)
         sa_t = sb.tile([P, 4], F32, name="sa_t")
         so_t = sb.tile([P, 2, 1], F32, name="so_t")
         tz_t = [sb.tile([P, E], F32, name="tz%d" % h) for h in range(2)]
 
-        for plane in (xts, wsc, xos, w2sc):
-            nc.vector.memset(plane[:].bitcast(I32), 0)
-        for plane in (wssc, wbsc):
-            nc.gpsimd.memset(plane[:].bitcast(I32), 0)
+        nc.vector.memset(wsc[:].bitcast(I32), 0)
+        nc.vector.memset(xts_pair[:], 0)
+        for pair in (w2sc, xos, osc):
+            nc.vector.memset(pair[:].bitcast(I32), 0)
 
         nc.sync.dma_start(l1[:], offs)
         nc.sync.dma_start(out=xtw[:].bitcast(I32), in_=xt_words[0].bitcast(I32))
-        load_plane(nc.scalar, xts, xt_scales)
+        load_half(nc.scalar, wsc, slice(0, R), w_scales, 0)
+        load_halves((nc.scalar, nc.sync), xts_pair, slice(0, T // 4), xt_scales)
+        load_half(nc.scalar, wsc, slice(0, R), w_scales, 1)
         nc.sync.dma_start(out=ww[:].bitcast(I32), in_=words32(w_words))
         nc.sync.dma_start(out=xow[:].bitcast(I32), in_=words32(xo_words))
-        load_plane(nc.scalar, wsc, w_scales)
         nc.sync.dma_start(l2[:], offs2)
-        load_plane(nc.sync, xos, xo_scales)
+        load_halves((nc.sync, nc.gpsimd), w2sc, slice(0, R), w2_scales)
         nc.sync.dma_start(out=w2w[:].bitcast(I32), in_=w2_words[0].bitcast(I32))
-        load_plane(nc.sync, w2sc, w2_scales)
-        nc.sync.dma_start(l3[:], offs3)
+        load_plane(nc.sync, xos, xo_scales)
         nc.sync.dma_start(l4[:], offs4)
-        for h in range(2):
-            nc.sync.dma_start(out=tz_t[h][:], in_=tz[P * h : P * (h + 1), :])
+        load_halves((nc.sync, nc.sync), osc, slice(0, N), ws_scales)
+        load_halves((nc.sync, nc.sync), osc, slice(N, 2 * N), wb_scales)
+        nc.sync.dma_start(l3[:], offs3)
+        nc.sync.dma_start(out=sa_t[:], in_=sa.rearrange("(p t) o -> p (t o)", t=4))
+        nc.sync.dma_start(out=tz_t[0][:], in_=tz[0:P, :])
         nc.sync.dma_start(out=wsw[:].bitcast(I32), in_=words32(ws_words))
         nc.sync.dma_start(out=wbw[:].bitcast(I32), in_=wb_words[0].bitcast(I32))
         nc.sync.dma_start(l5[:], offs5)
         with nc.allow_non_contiguous_dma(reason="one value a partition and half"):
             nc.sync.dma_start(out=so_t[:], in_=so.rearrange("(h p) o -> p h o", h=2))
-        load_plane(nc.sync, wbsc, wb_scales)
-        nc.gpsimd.dma_start(out=sa_t[:], in_=sa.rearrange("(p t) o -> p (t o)", t=4))
-        load_plane(nc.gpsimd, wssc, ws_scales)
+        nc.sync.dma_start(out=tz_t[1][:], in_=tz[P : 2 * P, :])
 
         xtw_g = sb.tile([P, J], U16, name="xtw_g", align_bytes=64)
         xts_g = sb.tile([P, J], U8, name="xts_g", align_bytes=64)
@@ -102,22 +117,29 @@ def tile_list_largestpicked_twotab_further_stepfloor_kernel(
         w2sc_d = sb.tile([P, 4, P], U8, name="w2sc_d", align_bytes=64)
 
         nc.vector.tensor_copy(xtw_g[:], xtw[:].indirect(l1[:]))
+        for half in range(2):
+            nc.vector.tensor_copy(out=xts[64 * half : 64 * (half + 1), :].bitcast(I32), in_=xts_pair[:, half, :])
+        lift(nc, wsc)
         nc.vector.tensor_copy(xts_g[:], xts[:].indirect(l1[:]))
-        deal(nc.scalar.copy, ww_d, ww, 4)
-        deal(nc.vector.tensor_copy, wsc_d, wsc, 16)
+        deal(nc.vector.tensor_copy, wsc_d, wsc[:, 0, :], 16)
+        deal(nc.scalar.copy, ww_d, ww[:], 4)
         a_ps = [ps.tile([P, 2, J], F32, name="a_ps%d" % u) for u in range(2)]
-        a_sb = [sb.tile([P, 2, J], F32, name="a_sb%d" % u) for u in range(2)]
         for t in range(4):
             nc.tensor.matmul_mx(
                 out=a_ps[t // 2][:, t % 2, :], lhsT=ww_d[:, t, :].bitcast(E4M3X4), lhsT_scale=wsc_d[:, t, :],
                 rhs=xtw_g[:].bitcast(E2M1X4), rhs_scale=xts_g[:], start=True, stop=True)
-        deal(nc.scalar.copy, w2w_d, w2w, 8)
+        deal(nc.scalar.copy, w2w_d, w2w[:], 8)
+        a_sb = [
+            sb.tile([P, 2, J], F32, name="a_sb0", tag="w2w_then_a", align_bytes=64),
+            sb.tile([P, 2, J], F32, name="a_sb1"),
+        ]
         for u in range(2):
             nc.scalar.copy(out=a_sb[u][:], in_=a_ps[u][:])
 
+        lift(nc, w2sc)
+        deal(nc.vector.tensor_copy, w2sc_d, w2sc[:, 0, :], 16)
         nc.vector.tensor_copy(xow_g[:], xow[:].indirect(l2[:]))
         nc.vector.tensor_copy(xos_g[:], xos[:].indirect(l2[:]))
-        deal(nc.vector.tensor_copy, w2sc_d, w2sc, 16)
         b_ps = [ps.tile([P, J], F32, name="b_ps%d" % t) for t in range(4)]
         g1 = [sb.tile([P, J], F32, name="g1_%d" % t) for t in range(4)]
         hid = sb.tile([P, 4, O], BF16, name="hid", align_bytes=64)
@@ -131,11 +153,12 @@ def tile_list_largestpicked_twotab_further_stepfloor_kernel(
 
         nc.vector.tensor_copy(xtw_g4[:], xtw[:].indirect(l4[:]))
         nc.vector.tensor_copy(xts_g4[:], xts[:].indirect(l4[:]))
+        lift(nc, osc)
         p_ps = [ps.tile([P, O], F32, name="p_ps%d" % h) for h in range(2)]
         for h in range(2):
             cols = slice(P * h, P * (h + 1))
             nc.tensor.matmul_mx(
-                out=p_ps[h][:], lhsT=wsw[:, cols].bitcast(E4M3X4), lhsT_scale=wssc[:, cols],
+                out=p_ps[h][:], lhsT=wsw[:, cols].bitcast(E4M3X4), lhsT_scale=osc[:, 0, cols],
                 rhs=xtw_g4[:].bitcast(E2M1X4), rhs_scale=xts_g4[:], start=True, stop=False)
 
         woven = sb.tile([P, O, 4], BF16, name="woven", align_bytes=64)
@@ -152,7 +175,7 @@ def tile_list_largestpicked_twotab_further_stepfloor_kernel(
         for h in range(2):
             cols = slice(P * h, P * (h + 1))
             nc.tensor.matmul_mx(
-                out=p_ps[h][:], lhsT=wbw[:, cols].bitcast(E2M1X4), lhsT_scale=wbsc[:, cols],
+                out=p_ps[h][:], lhsT=wbw[:, cols].bitcast(E2M1X4), lhsT_scale=osc[:, 0, N + P * h : N + P * (h + 1)],
                 rhs=hq[:].bitcast(E5M2X4), rhs_scale=hs[:], start=False, stop=True)
         for h, queue in enumerate((nc.sync, nc.scalar)):
             nc.vector.tensor_tensor(res[h][:], p_ps[h][:], floor_t[h][:], MAX)

@@ -19,8 +19,8 @@ K, T, Z, J, R, O, N, E = 512, 1024, 1024, 256, 512, 128, 256, 1024
 FLOPS = 2 * K * R * J * 2 + 2 * R * N * O + 2 * K * N * O
 
 
-def load_plane(queue, plane, scales):
-    for q in range(4):
+def load_plane(queues, plane, scales):
+    for q, queue in enumerate(queues):
         queue.dma_start(out=plane[32 * q : 32 * q + 4, :].bitcast(I32), in_=scales[0, 4 * q : 4 * q + 4, :].bitcast(I32))
 
 
@@ -62,7 +62,6 @@ def tile_list_largestpicked_twotab_further_stepfloor_kernel(
         l5 = sb.tile([P, O // 16], U16, name="l5")
         xtw = sb.tile([P, T], U16, name="xtw", align_bytes=64)
         xts = sb.tile([P, T], U8, name="xts", align_bytes=64)
-        xts_pair = sb.tile([64, 2, T // 4], I32, name="xts_pair")
         xow = sb.tile([P, Z], U32, name="xow", align_bytes=64)
         xos = sb.tile([P, Z], U8, name="xos", align_bytes=64)
         ww = sb.tile([P, R], U32, name="ww", align_bytes=64)
@@ -76,34 +75,31 @@ def tile_list_largestpicked_twotab_further_stepfloor_kernel(
         so_t = sb.tile([P, 2, 1], F32, name="so_t")
         tz_t = [sb.tile([P, E], F32, name="tz%d" % h) for h in range(2)]
 
-        nc.vector.memset(wsc[:].bitcast(I32), 0)
-        nc.vector.memset(xts_pair[:], 0)
-        for pair in (w2sc, xos, osc):
-            nc.vector.memset(pair[:].bitcast(I32), 0)
+        for plane in (wsc, xts, w2sc, xos, osc):
+            nc.vector.memset(plane[:].bitcast(I32), 0)
 
         nc.sync.dma_start(l1[:], offs)
         nc.sync.dma_start(out=xtw[:].bitcast(I32), in_=xt_words[0].bitcast(I32))
-        load_half(nc.scalar, wsc, slice(0, R), w_scales, 0)
-        load_halves((nc.scalar, nc.sync), xts_pair, slice(0, T // 4), xt_scales)
-        load_half(nc.scalar, wsc, slice(0, R), w_scales, 1)
+        load_halves((nc.scalar, nc.sync), wsc, slice(0, R), w_scales)
+        load_plane((nc.scalar, nc.scalar, nc.scalar, nc.sync), xts, xt_scales)
         nc.sync.dma_start(out=ww[:].bitcast(I32), in_=words32(w_words))
-        nc.sync.dma_start(out=xow[:].bitcast(I32), in_=words32(xo_words))
-        nc.sync.dma_start(l2[:], offs2)
         load_halves((nc.sync, nc.gpsimd), w2sc, slice(0, R), w2_scales)
+        nc.sync.dma_start(l2[:], offs2)
+        nc.sync.dma_start(out=xow[:].bitcast(I32), in_=words32(xo_words))
         nc.sync.dma_start(out=w2w[:].bitcast(I32), in_=w2_words[0].bitcast(I32))
-        load_plane(nc.sync, xos, xo_scales)
+        load_plane((nc.sync, nc.sync, nc.sync, nc.gpsimd), xos, xo_scales)
         nc.sync.dma_start(l4[:], offs4)
-        load_halves((nc.sync, nc.sync), osc, slice(0, N), ws_scales)
-        load_halves((nc.sync, nc.sync), osc, slice(N, 2 * N), wb_scales)
+        nc.sync.dma_start(out=tz_t[0][:], in_=tz[0:P, :])
+        load_halves((nc.gpsimd, nc.sync), osc, slice(0, N), ws_scales)
+        load_halves((nc.gpsimd, nc.sync), osc, slice(N, 2 * N), wb_scales)
         nc.sync.dma_start(l3[:], offs3)
         nc.sync.dma_start(out=sa_t[:], in_=sa.rearrange("(p t) o -> p (t o)", t=4))
-        nc.sync.dma_start(out=tz_t[0][:], in_=tz[0:P, :])
         nc.sync.dma_start(out=wsw[:].bitcast(I32), in_=words32(ws_words))
         nc.sync.dma_start(out=wbw[:].bitcast(I32), in_=wb_words[0].bitcast(I32))
+        nc.sync.dma_start(out=tz_t[1][:], in_=tz[P : 2 * P, :])
         nc.sync.dma_start(l5[:], offs5)
         with nc.allow_non_contiguous_dma(reason="one value a partition and half"):
             nc.sync.dma_start(out=so_t[:], in_=so.rearrange("(h p) o -> p h o", h=2))
-        nc.sync.dma_start(out=tz_t[1][:], in_=tz[P : 2 * P, :])
 
         xtw_g = sb.tile([P, J], U16, name="xtw_g", align_bytes=64)
         xts_g = sb.tile([P, J], U8, name="xts_g", align_bytes=64)
@@ -117,11 +113,9 @@ def tile_list_largestpicked_twotab_further_stepfloor_kernel(
         w2sc_d = sb.tile([P, 4, P], U8, name="w2sc_d", align_bytes=64)
 
         nc.vector.tensor_copy(xtw_g[:], xtw[:].indirect(l1[:]))
-        for half in range(2):
-            nc.vector.tensor_copy(out=xts[64 * half : 64 * (half + 1), :].bitcast(I32), in_=xts_pair[:, half, :])
         lift(nc, wsc)
-        nc.vector.tensor_copy(xts_g[:], xts[:].indirect(l1[:]))
         deal(nc.vector.tensor_copy, wsc_d, wsc[:, 0, :], 16)
+        nc.vector.tensor_copy(xts_g[:], xts[:].indirect(l1[:]))
         deal(nc.scalar.copy, ww_d, ww[:], 4)
         a_ps = [ps.tile([P, 2, J], F32, name="a_ps%d" % u) for u in range(2)]
         for t in range(4):

@@ -65,9 +65,8 @@ def tile_list_largestpicked_twotab_further_stepfloor_kernel(
         xow = sb.tile([P, Z], U32, name="xow", align_bytes=64)
         xos = sb.tile([P, Z], U8, name="xos", align_bytes=64)
         ww = sb.tile([P, R], U32, name="ww", align_bytes=64)
-        wsc = sb.tile([P, 2, R], U8, name="wsc", align_bytes=64)
+        wsc = sb.tile([P, 2, 2 * R], U8, name="wsc", align_bytes=64)
         w2w = sb.tile([P, R], U16, name="w2w", tag="w2w_then_a", align_bytes=64)
-        w2sc = sb.tile([P, 2, R], U8, name="w2sc", align_bytes=64)
         wbw = sb.tile([P, N], U16, name="wbw", align_bytes=64)
         wsw = sb.tile([P, N], U32, name="wsw", align_bytes=64)
         osc = sb.tile([P, 2, 2 * N], U8, name="osc", align_bytes=64)
@@ -75,15 +74,15 @@ def tile_list_largestpicked_twotab_further_stepfloor_kernel(
         so_t = sb.tile([P, 2, 1], F32, name="so_t")
         tz_t = [sb.tile([P, E], F32, name="tz%d" % h) for h in range(2)]
 
-        for plane in (wsc, xts, w2sc, xos, osc):
-            nc.vector.memset(plane[:].bitcast(I32), 0)
+        for plane in (xts[:], wsc[:, :, R : 2 * R], wsc[:, :, 0:R], xos[:], osc[:]):
+            nc.vector.memset(plane.bitcast(I32), 0)
 
         nc.sync.dma_start(l1[:], offs)
         nc.sync.dma_start(out=xtw[:].bitcast(I32), in_=xt_words[0].bitcast(I32))
-        load_halves((nc.scalar, nc.sync), wsc, slice(0, R), w_scales)
         load_plane((nc.scalar, nc.scalar, nc.scalar, nc.sync), xts, xt_scales)
+        load_halves((nc.scalar, nc.sync), wsc, slice(0, R), w_scales)
         nc.sync.dma_start(out=ww[:].bitcast(I32), in_=words32(w_words))
-        load_halves((nc.sync, nc.gpsimd), w2sc, slice(0, R), w2_scales)
+        load_halves((nc.sync, nc.gpsimd), wsc, slice(R, 2 * R), w2_scales)
         nc.sync.dma_start(l2[:], offs2)
         nc.sync.dma_start(out=xow[:].bitcast(I32), in_=words32(xo_words))
         nc.sync.dma_start(out=w2w[:].bitcast(I32), in_=w2_words[0].bitcast(I32))
@@ -113,9 +112,10 @@ def tile_list_largestpicked_twotab_further_stepfloor_kernel(
         w2sc_d = sb.tile([P, 4, P], U8, name="w2sc_d", align_bytes=64)
 
         nc.vector.tensor_copy(xtw_g[:], xtw[:].indirect(l1[:]))
-        lift(nc, wsc)
-        deal(nc.vector.tensor_copy, wsc_d, wsc[:, 0, :], 16)
         nc.vector.tensor_copy(xts_g[:], xts[:].indirect(l1[:]))
+        lift(nc, wsc)
+        deal(nc.vector.tensor_copy, wsc_d, wsc[:, 0, 0:R], 16)
+        deal(nc.vector.tensor_copy, w2sc_d, wsc[:, 0, R : 2 * R], 16)
         deal(nc.scalar.copy, ww_d, ww[:], 4)
         a_ps = [ps.tile([P, 2, J], F32, name="a_ps%d" % u) for u in range(2)]
         for t in range(4):
@@ -130,8 +130,6 @@ def tile_list_largestpicked_twotab_further_stepfloor_kernel(
         for u in range(2):
             nc.scalar.copy(out=a_sb[u][:], in_=a_ps[u][:])
 
-        lift(nc, w2sc)
-        deal(nc.vector.tensor_copy, w2sc_d, w2sc[:, 0, :], 16)
         nc.vector.tensor_copy(xow_g[:], xow[:].indirect(l2[:]))
         nc.vector.tensor_copy(xos_g[:], xos[:].indirect(l2[:]))
         b_ps = [ps.tile([P, J], F32, name="b_ps%d" % t) for t in range(4)]
@@ -143,7 +141,12 @@ def tile_list_largestpicked_twotab_further_stepfloor_kernel(
                 rhs=xow_g[:].bitcast(E4M3X4), rhs_scale=xos_g[:], start=True, stop=True)
         for t in range(4):
             nc.vector.tensor_tensor(g1[t][:], b_ps[t][:], a_sb[t // 2][:, t % 2, :], MAX)
-            nc.scalar.activation(out=hid[:, t, :], in_=g1[t][:].indirect(l3[:]), func=COPY, scale=sa_t[:, t : t + 1])
+            parts = 2 if t == 3 else 1
+            for u in range(parts):
+                n = O // parts
+                nc.scalar.activation(
+                    out=hid[:, t, n * u : n * (u + 1)], in_=g1[t][:].indirect(l3[:, n // 16 * u : n // 16 * (u + 1)]),
+                    func=COPY, scale=sa_t[:, t : t + 1])
 
         nc.vector.tensor_copy(xtw_g4[:], xtw[:].indirect(l4[:]))
         nc.vector.tensor_copy(xts_g4[:], xts[:].indirect(l4[:]))
@@ -155,12 +158,17 @@ def tile_list_largestpicked_twotab_further_stepfloor_kernel(
                 out=p_ps[h][:], lhsT=wsw[:, cols].bitcast(E4M3X4), lhsT_scale=osc[:, 0, cols],
                 rhs=xtw_g4[:].bitcast(E2M1X4), rhs_scale=xts_g4[:], start=True, stop=False)
 
-        woven = sb.tile([P, O, 4], BF16, name="woven", align_bytes=64)
-        nc.vector.tensor_copy(
-            out=woven[:].rearrange("p (c i) t -> p c t i", i=4), in_=hid[:].rearrange("p t (c i) -> p c t i", i=4))
+        woven = [sb.tile([P, O // 2, 4], BF16, name="woven%d" % u, align_bytes=64) for u in range(2)]
+        for u in range(2):
+            nc.vector.tensor_copy(
+                out=woven[u][:].rearrange("p (c i) t -> p c t i", i=4),
+                in_=hid[:, :, 64 * u : 64 * (u + 1)].rearrange("p t (c i) -> p c t i", i=4))
         hq = sb.tile([P, O], U32, name="hq", align_bytes=64)
         hs = sb.tile([P, O], U8, name="hs", align_bytes=64)
-        nc.vector.quantize_mx(out=hq[:].bitcast(E5M2X4), scales=hs[:], in_=woven[:].rearrange("p o t -> p (o t)"))
+        for u in range(2):
+            places = slice(64 * u, 64 * (u + 1))
+            nc.vector.quantize_mx(
+                out=hq[:, places].bitcast(E5M2X4), scales=hs[:, places], in_=woven[u][:].rearrange("p o t -> p (o t)"))
 
         floor_t = [sb.tile([P, O], F32, name="floor%d" % h) for h in range(2)]
         res = [sb.tile([P, O], F32, name="res%d" % h) for h in range(2)]

from contextlib import ExitStack

import concourse.mybir as mybir

F32 = mybir.dt.float32
BF16 = mybir.dt.bfloat16
I32 = mybir.dt.int32
U32 = mybir.dt.uint32
U16 = mybir.dt.uint16
U8 = mybir.dt.uint8
E4M3X4 = mybir.dt.float8_e4m3fn_x4
E5M2X4 = mybir.dt.float8_e5m2_x4
E2M1X4 = mybir.dt.float4_e2m1fn_x4
COPY = mybir.ActivationFunctionType.Copy
MAX = mybir.AluOpType.max

P = 128
K, T, Z, J, R, O, N, E = 512, 1024, 1024, 256, 512, 128, 256, 1024
FLOPS = 2 * K * R * J * 2 + 2 * R * N * O + 2 * K * N * O


def load_plane(queues, plane, scales):
    for q, queue in enumerate(queues):
        queue.dma_start(out=plane[32 * q : 32 * q + 4, :].bitcast(I32), in_=scales[0, 4 * q : 4 * q + 4, :].bitcast(I32))


def load_half(queue, pair, cols, scales, q):
    by_quadrant = scales[0].rearrange("(b q r) c -> q r b c", b=2, q=2)
    queue.dma_start(out=pair[32 * q : 32 * q + 4, :, cols].bitcast(I32), in_=by_quadrant[q].bitcast(I32))


def load_halves(queues, pair, cols, scales):
    for q, queue in enumerate(queues):
        load_half(queue, pair, cols, scales, q)


def lift(nc, pair):
    nc.vector.tensor_copy(out=pair[64:128, 0, :].bitcast(I32), in_=pair[0:64, 1, :].bitcast(I32))


def words32(words):
    return words[0].rearrange("p n t -> p (n t)").bitcast(I32)


def deal(copy, dealt, natural, run):
    copy(out=dealt[:].rearrange("p t (b i) -> p b t i", i=run), in_=natural.rearrange("p (b i t) -> p b t i", i=run, t=4))


def tile_list_largestpicked_twotab_further_stepfloor_kernel(
    tc, xt_words, xt_scales, w_words, w_scales, xo_words, xo_scales, w2_words, w2_scales, sa,
    wb_words, wb_scales, ws_words, ws_scales, tz, so, offs, offs2, offs3, offs4, offs5, out,
):
    nc = tc.nc
    with ExitStack() as ctx:
        sb = ctx.enter_context(tc.tile_pool(name="sb", bufs=1))
        ps = ctx.enter_context(tc.psum_pool(name="ps", bufs=1))

        l1 = sb.tile([P, J // 16], U16, name="l1")
        l2 = sb.tile([P, J // 16], U16, name="l2")
        l3 = sb.tile([P, O // 16], U16, name="l3")
        l4 = sb.tile([P, O // 16], U16, name="l4")
        l5 = sb.tile([P, O // 16], U16, name="l5")
        xtw = sb.tile([P, T], U16, name="xtw", align_bytes=64)
        xts = sb.tile([P, T], U8, name="xts", align_bytes=64)
        xow = sb.tile([P, Z], U32, name="xow", align_bytes=64)
        xos = sb.tile([P, Z], U8, name="xos", align_bytes=64)
        ww = sb.tile([P, R], U32, name="ww", align_bytes=64)
        wsc = sb.tile([P, 2, 2 * R], U8, name="wsc", align_bytes=64)
        w2w = sb.tile([P, R], U16, name="w2w", tag="w2w_then_a", align_bytes=64)
        wbw = sb.tile([P, N], U16, name="wbw", align_bytes=64)
        wsw = sb.tile([P, N], U32, name="wsw", align_bytes=64)
        osc = sb.tile([P, 2, 2 * N], U8, name="osc", align_bytes=64)
        sa_t = sb.tile([P, 4], F32, name="sa_t")
        so_t = sb.tile([P, 2, 1], F32, name="so_t")
        tz_t = [sb.tile([P, E], F32, name="tz%d" % h) for h in range(2)]

        for plane in (xts[:], wsc[:, :, R : 2 * R], wsc[:, :, 0:R], xos[:], osc[:]):
            nc.vector.memset(plane.bitcast(I32), 0)

        nc.sync.dma_start(l1[:], offs)
        nc.sync.dma_start(out=xtw[:].bitcast(I32), in_=xt_words[0].bitcast(I32))
        load_plane((nc.scalar, nc.scalar, nc.scalar, nc.sync), xts, xt_scales)
        load_halves((nc.scalar, nc.sync), wsc, slice(0, R), w_scales)
        nc.sync.dma_start(out=ww[:].bitcast(I32), in_=words32(w_words))
        load_halves((nc.sync, nc.gpsimd), wsc, slice(R, 2 * R), w2_scales)
        nc.sync.dma_start(l2[:], offs2)
        nc.sync.dma_start(out=xow[:].bitcast(I32), in_=words32(xo_words))
        nc.sync.dma_start(out=w2w[:].bitcast(I32), in_=w2_words[0].bitcast(I32))
        load_plane((nc.sync, nc.sync, nc.sync, nc.gpsimd), xos, xo_scales)
        nc.sync.dma_start(l4[:], offs4)
        nc.sync.dma_start(out=tz_t[0][:], in_=tz[0:P, :])
        load_halves((nc.gpsimd, nc.sync), osc, slice(0, N), ws_scales)
        load_halves((nc.gpsimd, nc.sync), osc, slice(N, 2 * N), wb_scales)
        nc.sync.dma_start(l3[:], offs3)
        nc.sync.dma_start(out=sa_t[:], in_=sa.rearrange("(p t) o -> p (t o)", t=4))
        nc.sync.dma_start(out=wsw[:].bitcast(I32), in_=words32(ws_words))
        nc.sync.dma_start(out=wbw[:].bitcast(I32), in_=wb_words[0].bitcast(I32))
        nc.sync.dma_start(out=tz_t[1][:], in_=tz[P : 2 * P, :])
        nc.sync.dma_start(l5[:], offs5)
        with nc.allow_non_contiguous_dma(reason="one value a partition and half"):
            nc.sync.dma_start(out=so_t[:], in_=so.rearrange("(h p) o -> p h o", h=2))

        xtw_g = sb.tile([P, J], U16, name="xtw_g", align_bytes=64)
        xts_g = sb.tile([P, J], U8, name="xts_g", align_bytes=64)
        xow_g = sb.tile([P, J], U32, name="xow_g", align_bytes=64)
        xos_g = sb.tile([P, J], U8, name="xos_g", align_bytes=64)
        xtw_g4 = sb.tile([P, O], U16, name="xtw_g4", align_bytes=64)
        xts_g4 = sb.tile([P, O], U8, name="xts_g4", align_bytes=64)
        ww_d = sb.tile([P, 4, P], U32, name="ww_d", align_bytes=64)
        wsc_d = sb.tile([P, 4, P], U8, name="wsc_d", align_bytes=64)
        w2w_d = sb.tile([P, 4, P], U16, name="w2w_d", align_bytes=64)
        w2sc_d = sb.tile([P, 4, P], U8, name="w2sc_d", align_bytes=64)

        nc.vector.tensor_copy(xtw_g[:], xtw[:].indirect(l1[:]))
        nc.vector.tensor_copy(xts_g[:], xts[:].indirect(l1[:]))
        lift(nc, wsc)
        deal(nc.vector.tensor_copy, wsc_d, wsc[:, 0, 0:R], 16)
        deal(nc.vector.tensor_copy, w2sc_d, wsc[:, 0, R : 2 * R], 16)
        deal(nc.scalar.copy, ww_d, ww[:], 4)
        a_ps = [ps.tile([P, 2, J], F32, name="a_ps%d" % u) for u in range(2)]
        for t in range(4):
            nc.tensor.matmul_mx(
                out=a_ps[t // 2][:, t % 2, :], lhsT=ww_d[:, t, :].bitcast(E4M3X4), lhsT_scale=wsc_d[:, t, :],
                rhs=xtw_g[:].bitcast(E2M1X4), rhs_scale=xts_g[:], start=True, stop=True)
        deal(nc.scalar.copy, w2w_d, w2w[:], 8)
        a_sb = [
            sb.tile([P, 2, J], F32, name="a_sb0", tag="w2w_then_a", align_bytes=64),
            sb.tile([P, 2, J], F32, name="a_sb1"),
        ]
        for u in range(2):
            nc.scalar.copy(out=a_sb[u][:], in_=a_ps[u][:])

        nc.vector.tensor_copy(xow_g[:], xow[:].indirect(l2[:]))
        nc.vector.tensor_copy(xos_g[:], xos[:].indirect(l2[:]))
        b_ps = [ps.tile([P, J], F32, name="b_ps%d" % t) for t in range(4)]
        g1 = [sb.tile([P, J], F32, name="g1_%d" % t) for t in range(4)]
        hid = sb.tile([P, 4, O], BF16, name="hid", align_bytes=64)
        for t in range(4):
            nc.tensor.matmul_mx(
                out=b_ps[t][:], lhsT=w2w_d[:, t, :].bitcast(E2M1X4), lhsT_scale=w2sc_d[:, t, :],
                rhs=xow_g[:].bitcast(E4M3X4), rhs_scale=xos_g[:], start=True, stop=True)
        for t in range(4):
            nc.vector.tensor_tensor(g1[t][:], b_ps[t][:], a_sb[t // 2][:, t % 2, :], MAX)
            parts = 2 if t == 3 else 1
            for u in range(parts):
                n = O // parts
                nc.scalar.activation(
                    out=hid[:, t, n * u : n * (u + 1)], in_=g1[t][:].indirect(l3[:, n // 16 * u : n // 16 * (u + 1)]),
                    func=COPY, scale=sa_t[:, t : t + 1])

        nc.vector.tensor_copy(xtw_g4[:], xtw[:].indirect(l4[:]))
        nc.vector.tensor_copy(xts_g4[:], xts[:].indirect(l4[:]))
        lift(nc, osc)
        p_ps = [ps.tile([P, O], F32, name="p_ps%d" % h) for h in range(2)]
        for h in range(2):
            cols = slice(P * h, P * (h + 1))
            nc.tensor.matmul_mx(
                out=p_ps[h][:], lhsT=wsw[:, cols].bitcast(E4M3X4), lhsT_scale=osc[:, 0, cols],
                rhs=xtw_g4[:].bitcast(E2M1X4), rhs_scale=xts_g4[:], start=True, stop=False)

        woven = [sb.tile([P, O // 2, 4], BF16, name="woven%d" % u, align_bytes=64) for u in range(2)]
        for u in range(2):
            nc.vector.tensor_copy(
                out=woven[u][:].rearrange("p (c i) t -> p c t i", i=4),
                in_=hid[:, :, 64 * u : 64 * (u + 1)].rearrange("p t (c i) -> p c t i", i=4))
        hq = sb.tile([P, O], U32, name="hq", align_bytes=64)
        hs = sb.tile([P, O], U8, name="hs", align_bytes=64)
        for u in range(2):
            places = slice(64 * u, 64 * (u + 1))
            nc.vector.quantize_mx(
                out=hq[:, places].bitcast(E5M2X4), scales=hs[:, places], in_=woven[u][:].rearrange("p o t -> p (o t)"))

        floor_t = [sb.tile([P, O], F32, name="floor%d" % h) for h in range(2)]
        res = [sb.tile([P, O], F32, name="res%d" % h) for h in range(2)]
        for h in range(2):
            nc.scalar.activation(out=floor_t[h][:], in_=tz_t[h][:].indirect(l5[:]), func=COPY, scale=so_t[:, h, :])
        for h in range(2):
            cols = slice(P * h, P * (h + 1))
            nc.tensor.matmul_mx(
                out=p_ps[h][:], lhsT=wbw[:, cols].bitcast(E2M1X4), lhsT_scale=osc[:, 0, N + P * h : N + P * (h + 1)],
                rhs=hq[:].bitcast(E5M2X4), rhs_scale=hs[:], start=False, stop=True)
        for h, queue in enumerate((nc.sync, nc.scalar)):
            nc.vector.tensor_tensor(res[h][:], p_ps[h][:], floor_t[h][:], MAX)
            queue.dma_start(out=out[P * h : P * (h + 1), :], in_=res[h][:])
